import numpy as np
CORES = [5,13,21,29,133,141,149,157,261,269,277,285,389,397,405,413]
N = 16
ROOT = 10
def setup_inputs(rng):
    return {"x": rng.standard_normal((N, 128, 1024), dtype=np.float32)}
def reference(x):
    return {"y": np.broadcast_to(x[ROOT], x.shape)}

@@ -1,0 +1,102 @@
+import concourse.bass as bass
+import comms_topo
+ROOT = 277
+P = 32
+NW = 4
+PW = P // NW
+W = 1024 // P
+R = 128 // P
+K4 = (2, 3, 6, 7)
+HELP = (0, 2, 4, 6)
+NEAR = ((3, 0), (3, 2), (3, 4), (3, 6), (2, 0), (2, 4), (2, 6), (2, 8))
+FAR = ((1, 2), (1, 0), (1, 4), (1, 6), (1, 8), (1, 10), (1, 12), (1, 14))
+SCRATCH = {'d': ('dram', [P, 128, W], 'float32')}
+SEMAPHORES = ['a0', 'a1', 'a2', 'a3', 'l0', 'l1', 'l2', 'l3', 'sent', 'st']
+
+def wc(h, c, k):
+    return h * 128 + c * 8 + k
+
+def plan():
+    kids, sched = ({}, {})
+    for h in range(4):
+        for c in range(4):
+            sched[wc(h, c, 5)] = [list(range(PW * w, PW * w + PW)) for w in range(NW)]
+    sched[ROOT] = [list(range(0, P // 2)), list(range(P // 2, P))]
+    for k in HELP:
+        sched[wc(2, 2, k)] = [[] for w in range(NW)]
+    for p in range(P):
+        w, j = divmod(p, PW)
+        helper = wc(2, 2, HELP[j % 4])
+        kids[ROOT, p] = [helper]
+        sched[helper][w].append(p)
+        k = K4[(w + j) % 4]
+        far, near = (wc(FAR[j][0], FAR[j][1], k), wc(NEAR[j][0], NEAR[j][1], k))
+        kids[helper, p] = [far, near]
+        for refl, hosts in ((far, (1, 0)), (near, (2, 3))):
+            ranks = [wc(h, c, 5) for h in hosts for c in range(4) if wc(h, c, 5) != ROOT]
+            s = p % len(ranks)
+            kids[refl, p] = ranks[s:] + ranks[:s]
+            sched[refl] = [[p]]
+    return (kids, sched)
+
+def transfers(core, grp, kids):
+    send = [p for p in grp if kids.get((core, p))]
+    if not send:
+        return []
+    avail = 65535
+    for p in send:
+        for d in kids[core, p]:
+            avail &= comms_topo.mask(core, d)
+    n = 16 if avail == 65535 else 8
+    e = 1
+    while e * 2 * len(send) <= n:
+        e *= 2
+    return [(p, kids[core, p], (1 << e) - 1 << i * e, e) for i, p in enumerate(send)]
+
+def rank_program(g, core, T, topo):
+    kids, sched = plan()
+    my = sched.get(core)
+    if not my:
+        return
+    inc = {}
+    for src, groups in sched.items():
+        for grp in groups:
+            for p, dsts, m, e in transfers(src, grp, kids):
+                if core in dsts:
+                    inc[p] = e
+    A = [T.sem.a0, T.sem.a1, T.sem.a2, T.sem.a3]
+    L = [T.sem.l0, T.sem.l1, T.sem.l2, T.sem.l3]
+    is_root = core == ROOT
+    is_rank = T.rank_of(core) is not None
+    sent = stores = 0
+    if is_root:
+        for gi, grp in enumerate(my):
+            lo, hi = (grp[0], grp[-1] + 1)
+            g.dma_start(T.d[lo:hi], T.x[lo * R:hi * R, :]).then_inc(L[gi], 16)
+    for gi, grp in enumerate(my):
+        if is_root:
+            g.wait_ge(L[gi], 16)
+        else:
+            g.wait_ge(A[grp[0] // PW], sum((inc[p] for p in grp)))
+        trs = transfers(core, grp, kids)
+        if trs:
+            calls = []
+            for p, dsts, m, e in trs:
+                ids = []
+                for d in dsts:
+                    rid, pid = topo.addr(d, core)
+                    ids.append(bass.DstId(rid=rid, pnc=pid))
+                calls.append(bass.RemoteDMATransfer(dst_ids=ids, dma_engine_mask=m, remote_sem=A[p // PW], srcs=[T.d[p]], dsts=[T.d[p] for d in dsts]))
+                sent += e
+            g.remote_dma_fused(calls, local_sem=T.sem.sent)
+        if is_rank and (not is_root):
+            lo, hi = (grp[0], grp[-1] + 1)
+            g.dma_start(T.y[lo * R:hi * R, :], T.d[lo:hi]).then_inc(T.sem.st, 16)
+            stores += 1
+    if is_root:
+        g.dma_start(T.y[:, :], T.x[:, :]).then_inc(T.sem.st, 16)
+        stores += 1
+    if sent:
+        g.wait_ge(T.sem.sent, sent)
+    if stores:
+        g.wait_ge(T.sem.st, 16 * stores)

@@ -69,10 +69,11 @@ def rank_program(g, core, T, topo):
     is_root = core == ROOT
     is_rank = T.rank_of(core) is not None
     sent = stores = 0
+    Q = [g.sync, g.scalar]
     if is_root:
         for gi, grp in enumerate(my):
             lo, hi = (grp[0], grp[-1] + 1)
-            g.dma_start(T.d[lo:hi], T.x[lo * R:hi * R, :]).then_inc(L[gi], 16)
+            Q[gi % 2].dma_start(T.d[lo:hi], T.x[lo * R:hi * R, :]).then_inc(L[gi], 16)
     for gi, grp in enumerate(my):
         if is_root:
             g.wait_ge(L[gi], 16)
@@ -91,10 +92,13 @@ def rank_program(g, core, T, topo):
             g.remote_dma_fused(calls, local_sem=T.sem.sent)
         if is_rank and (not is_root):
             lo, hi = (grp[0], grp[-1] + 1)
-            g.dma_start(T.y[lo * R:hi * R, :], T.d[lo:hi]).then_inc(T.sem.st, 16)
+            q = Q[gi % 2]
+            q.wait_ge(A[grp[0] // PW], sum((inc[p] for p in grp)))
+            q.dma_start(T.y[lo * R:hi * R, :], T.d[lo:hi]).then_inc(T.sem.st, 16)
             stores += 1
     if is_root:
-        g.dma_start(T.y[:, :], T.x[:, :]).then_inc(T.sem.st, 16)
+        g.sync.wait_ge(T.sem.sent, sent)
+        g.sync.dma_start(T.y[:, :], T.x[:, :]).then_inc(T.sem.st, 16)
         stores += 1
     if sent:
         g.wait_ge(T.sem.sent, sent)

@@ -2,40 +2,34 @@ import concourse.bass as bass
 import comms_topo
 ROOT = 277
 P = 32
-NW = 4
-PW = P // NW
 W = 1024 // P
 R = 128 // P
-K4 = (2, 3, 6, 7)
-HELP = (0, 2, 4, 6)
-NEAR = ((3, 0), (3, 2), (3, 4), (3, 6), (2, 0), (2, 4), (2, 6), (2, 8))
-FAR = ((1, 2), (1, 0), (1, 4), (1, 6), (1, 8), (1, 10), (1, 12), (1, 14))
+WAVES = ((0, 8, 'D'), (8, 16, 'D'), (16, 24, 'D'), (24, 32, 'D'))
+NW = len(WAVES)
+WAVE_OF = {p: w for w, (lo, hi, t) in enumerate(WAVES) for p in range(lo, hi)}
+XCH = tuple((3, c) for c in range(0, 16, 2)) + tuple((2, c) for c in range(0, 16, 2) if c != 2)
+CABLED = {2: 1, 3: 0}
 SCRATCH = {'d': ('dram', [P, 128, W], 'float32')}
-SEMAPHORES = ['a0', 'a1', 'a2', 'a3', 'l0', 'l1', 'l2', 'l3', 'sent', 'st']
+SEMAPHORES = ['a0', 'a1', 'a2', 'a3', 'a4', 'a5', 'l0', 'l1', 'l2', 'l3', 'l4', 'l5', 'sent', 'st']
 
 def wc(h, c, k):
     return h * 128 + c * 8 + k
 
 def plan():
     kids, sched = ({}, {})
+    waves = [list(range(lo, hi)) for lo, hi, t in WAVES]
     for h in range(4):
         for c in range(4):
-            sched[wc(h, c, 5)] = [list(range(PW * w, PW * w + PW)) for w in range(NW)]
-    sched[ROOT] = [list(range(0, P // 2)), list(range(P // 2, P))]
-    for k in HELP:
-        sched[wc(2, 2, k)] = [[] for w in range(NW)]
+            sched[wc(h, c, 5)] = waves
     for p in range(P):
-        w, j = divmod(p, PW)
-        helper = wc(2, 2, HELP[j % 4])
-        kids[ROOT, p] = [helper]
-        sched[helper][w].append(p)
-        k = K4[(w + j) % 4]
-        far, near = (wc(FAR[j][0], FAR[j][1], k), wc(NEAR[j][0], NEAR[j][1], k))
-        kids[helper, p] = [far, near]
-        for refl, hosts in ((far, (1, 0)), (near, (2, 3))):
+        h, c = XCH[p % 15]
+        k = (2, 6, 3)[p // 15]
+        near, far = (wc(h, c, k), wc(CABLED[h], c, k))
+        kids[ROOT, p] = [near]
+        for refl, hosts, first in ((far, (1, 0), []), (near, (2, 3), [far])):
             ranks = [wc(h, c, 5) for h in hosts for c in range(4) if wc(h, c, 5) != ROOT]
             s = p % len(ranks)
-            kids[refl, p] = ranks[s:] + ranks[:s]
+            kids[refl, p] = first + ranks[s:] + ranks[:s]
             sched[refl] = [[p]]
     return (kids, sched)
 
@@ -64,8 +58,8 @@ def rank_program(g, core, T, topo):
             for p, dsts, m, e in transfers(src, grp, kids):
                 if core in dsts:
                     inc[p] = e
-    A = [T.sem.a0, T.sem.a1, T.sem.a2, T.sem.a3]
-    L = [T.sem.l0, T.sem.l1, T.sem.l2, T.sem.l3]
+    A = [T.sem.a0, T.sem.a1, T.sem.a2, T.sem.a3, T.sem.a4, T.sem.a5]
+    L = [T.sem.l0, T.sem.l1, T.sem.l2, T.sem.l3, T.sem.l4, T.sem.l5]
     is_root = core == ROOT
     is_rank = T.rank_of(core) is not None
     sent = stores = 0
@@ -75,10 +69,11 @@ def rank_program(g, core, T, topo):
             lo, hi = (grp[0], grp[-1] + 1)
             Q[gi % 2].dma_start(T.d[lo:hi], T.x[lo * R:hi * R, :]).then_inc(L[gi], 16)
     for gi, grp in enumerate(my):
+        arrive = A[WAVE_OF[grp[0]]]
         if is_root:
             g.wait_ge(L[gi], 16)
         else:
-            g.wait_ge(A[grp[0] // PW], sum((inc[p] for p in grp)))
+            g.wait_ge(arrive, sum((inc[p] for p in grp)))
         trs = transfers(core, grp, kids)
         if trs:
             calls = []
@@ -87,13 +82,13 @@ def rank_program(g, core, T, topo):
                 for d in dsts:
                     rid, pid = topo.addr(d, core)
                     ids.append(bass.DstId(rid=rid, pnc=pid))
-                calls.append(bass.RemoteDMATransfer(dst_ids=ids, dma_engine_mask=m, remote_sem=A[p // PW], srcs=[T.d[p]], dsts=[T.d[p] for d in dsts]))
+                calls.append(bass.RemoteDMATransfer(dst_ids=ids, dma_engine_mask=m, remote_sem=A[WAVE_OF[p]], srcs=[T.d[p]], dsts=[T.d[p] for d in dsts]))
                 sent += e
             g.remote_dma_fused(calls, local_sem=T.sem.sent)
         if is_rank and (not is_root):
             lo, hi = (grp[0], grp[-1] + 1)
             q = Q[gi % 2]
-            q.wait_ge(A[grp[0] // PW], sum((inc[p] for p in grp)))
+            q.wait_ge(arrive, sum((inc[p] for p in grp)))
             q.dma_start(T.y[lo * R:hi * R, :], T.d[lo:hi]).then_inc(T.sem.st, 16)
             stores += 1
     if is_root:

@@ -4,7 +4,8 @@ ROOT = 277
 P = 32
 W = 1024 // P
 R = 128 // P
-WAVES = ((0, 8, 'D'), (8, 16, 'D'), (16, 24, 'D'), (24, 32, 'D'))
+WAVES = ((0, 8, 'H'), (8, 16, 'H'), (16, 24, 'D'), (24, 32, 'D'))
+HELP = (0, 1, 2, 3)
 NW = len(WAVES)
 WAVE_OF = {p: w for w, (lo, hi, t) in enumerate(WAVES) for p in range(lo, hi)}
 XCH = tuple((3, c) for c in range(0, 16, 2)) + tuple((2, c) for c in range(0, 16, 2) if c != 2)
@@ -25,12 +26,20 @@ def plan():
         h, c = XCH[p % 15]
         k = (2, 6, 3)[p // 15]
         near, far = (wc(h, c, k), wc(CABLED[h], c, k))
-        kids[ROOT, p] = [near]
+        if WAVES[WAVE_OF[p]][2] == 'H':
+            helper = wc(2, 2, HELP[p % 4])
+            kids[ROOT, p] = [helper]
+            kids[helper, p] = [near]
+            sched.setdefault(helper, [[] for w in WAVES])[WAVE_OF[p]].append(p)
+        else:
+            kids[ROOT, p] = [near]
         for refl, hosts, first in ((far, (1, 0), []), (near, (2, 3), [far])):
             ranks = [wc(h, c, 5) for h in hosts for c in range(4) if wc(h, c, 5) != ROOT]
             s = p % len(ranks)
             kids[refl, p] = first + ranks[s:] + ranks[:s]
             sched[refl] = [[p]]
+    for k in HELP:
+        sched[wc(2, 2, k)] = [grp for grp in sched[wc(2, 2, k)] if grp]
     return (kids, sched)
 
 def transfers(core, grp, kids):
@@ -87,7 +96,7 @@ def rank_program(g, core, T, topo):
             g.remote_dma_fused(calls, local_sem=T.sem.sent)
         if is_rank and (not is_root):
             lo, hi = (grp[0], grp[-1] + 1)
-            q = Q[gi % 2]
+            q = Q[WAVES[gi][2] == 'H']
             q.wait_ge(arrive, sum((inc[p] for p in grp)))
             q.dma_start(T.y[lo * R:hi * R, :], T.d[lo:hi]).then_inc(T.sem.st, 16)
             stores += 1

@@ -4,57 +4,66 @@ ROOT = 277
 P = 32
 W = 1024 // P
 R = 128 // P
-WAVES = ((0, 8, 'H'), (8, 16, 'H'), (16, 24, 'D'), (24, 32, 'D'))
+WAVES = ((0, 8), (8, 16), (16, 26), (26, 32))
+PATH = 'HHHHHHHH' + 'DDDDDDDD' + 'DDDDDDDDCC' + 'DDDDCC'
+STORE_Q = (1, 0, 1, 0)
+STORE_ORDER = (1, 2, 3, 0)
 HELP = (0, 1, 2, 3)
 NW = len(WAVES)
-WAVE_OF = {p: w for w, (lo, hi, t) in enumerate(WAVES) for p in range(lo, hi)}
+WAVE_OF = {p: w for w, (lo, hi) in enumerate(WAVES) for p in range(lo, hi)}
 XCH = tuple((3, c) for c in range(0, 16, 2)) + tuple((2, c) for c in range(0, 16, 2) if c != 2)
 CABLED = {2: 1, 3: 0}
 SCRATCH = {'d': ('dram', [P, 128, W], 'float32')}
-SEMAPHORES = ['a0', 'a1', 'a2', 'a3', 'a4', 'a5', 'l0', 'l1', 'l2', 'l3', 'l4', 'l5', 'sent', 'st']
+SEMAPHORES = ['a0', 'a1', 'a2', 'a3', 'l0', 'l1', 'l2', 'l3', 'sent', 'st']
 
 def wc(h, c, k):
     return h * 128 + c * 8 + k
 
 def plan():
-    kids, sched = ({}, {})
-    waves = [list(range(lo, hi)) for lo, hi, t in WAVES]
+    kids, by = ({}, {})
+    def job(core, p):
+        by.setdefault(core, {}).setdefault(WAVE_OF[p], []).append(p)
     for h in range(4):
         for c in range(4):
-            sched[wc(h, c, 5)] = waves
+            for p in range(P):
+                job(wc(h, c, 5), p)
+    nx = nc = 0
     for p in range(P):
-        h, c = XCH[p % 15]
-        k = (2, 6, 3)[p // 15]
+        if PATH[p] == 'C':
+            h, c, k = (2, 2, (2, 6, 3, 7)[nc])
+            nc += 1
+        else:
+            h, c = XCH[nx % 15]
+            k = (2, 6)[nx // 15]
+            nx += 1
         near, far = (wc(h, c, k), wc(CABLED[h], c, k))
-        if WAVES[WAVE_OF[p]][2] == 'H':
+        if PATH[p] == 'H':
             helper = wc(2, 2, HELP[p % 4])
             kids[ROOT, p] = [helper]
             kids[helper, p] = [near]
-            sched.setdefault(helper, [[] for w in WAVES])[WAVE_OF[p]].append(p)
+            job(helper, p)
         else:
             kids[ROOT, p] = [near]
         for refl, hosts, first in ((far, (1, 0), []), (near, (2, 3), [far])):
             ranks = [wc(h, c, 5) for h in hosts for c in range(4) if wc(h, c, 5) != ROOT]
             s = p % len(ranks)
             kids[refl, p] = first + ranks[s:] + ranks[:s]
-            sched[refl] = [[p]]
-    for k in HELP:
-        sched[wc(2, 2, k)] = [grp for grp in sched[wc(2, 2, k)] if grp]
+            job(refl, p)
+    sched = {core: [ws[w] for w in sorted(ws)] for core, ws in by.items()}
     return (kids, sched)
 
 def transfers(core, grp, kids):
     send = [p for p in grp if kids.get((core, p))]
-    if not send:
-        return []
-    avail = 65535
-    for p in send:
-        for d in kids[core, p]:
-            avail &= comms_topo.mask(core, d)
-    n = 16 if avail == 65535 else 8
-    e = 1
-    while e * 2 * len(send) <= n:
-        e *= 2
-    return [(p, kids[core, p], (1 << e) - 1 << i * e, e) for i, p in enumerate(send)]
+    off = [p for p in send if any(comms_topo.mask(core, d) != 65535 for d in kids[core, p])]
+    on = [p for p in send if p not in off]
+    out = []
+    for ps, n, base in ((off, 8, 0), (on, 8 if off else 16, 8 if off else 0)):
+        if ps:
+            e = 1
+            while e * 2 * len(ps) <= n:
+                e *= 2
+            out += [(p, kids[core, p], (1 << e) - 1 << base + i * e, e) for i, p in enumerate(ps)]
+    return out
 
 def rank_program(g, core, T, topo):
     kids, sched = plan()
@@ -67,40 +76,38 @@ def rank_program(g, core, T, topo):
             for p, dsts, m, e in transfers(src, grp, kids):
                 if core in dsts:
                     inc[p] = e
-    A = [T.sem.a0, T.sem.a1, T.sem.a2, T.sem.a3, T.sem.a4, T.sem.a5]
-    L = [T.sem.l0, T.sem.l1, T.sem.l2, T.sem.l3, T.sem.l4, T.sem.l5]
-    is_root = core == ROOT
-    is_rank = T.rank_of(core) is not None
-    sent = stores = 0
+    A = [T.sem.a0, T.sem.a1, T.sem.a2, T.sem.a3]
+    L = [T.sem.l0, T.sem.l1, T.sem.l2, T.sem.l3]
     Q = [g.sync, g.scalar]
-    if is_root:
+    sent = stores = 0
+    if core == ROOT:
         for gi, grp in enumerate(my):
             lo, hi = (grp[0], grp[-1] + 1)
             Q[gi % 2].dma_start(T.d[lo:hi], T.x[lo * R:hi * R, :]).then_inc(L[gi], 16)
-    for gi, grp in enumerate(my):
-        arrive = A[WAVE_OF[grp[0]]]
-        if is_root:
-            g.wait_ge(L[gi], 16)
-        else:
-            g.wait_ge(arrive, sum((inc[p] for p in grp)))
-        trs = transfers(core, grp, kids)
-        if trs:
-            calls = []
-            for p, dsts, m, e in trs:
-                ids = []
-                for d in dsts:
-                    rid, pid = topo.addr(d, core)
-                    ids.append(bass.DstId(rid=rid, pnc=pid))
-                calls.append(bass.RemoteDMATransfer(dst_ids=ids, dma_engine_mask=m, remote_sem=A[WAVE_OF[p]], srcs=[T.d[p]], dsts=[T.d[p] for d in dsts]))
-                sent += e
-            g.remote_dma_fused(calls, local_sem=T.sem.sent)
-        if is_rank and (not is_root):
+    elif T.rank_of(core) is not None:
+        for gi in STORE_ORDER:
+            grp = my[gi]
             lo, hi = (grp[0], grp[-1] + 1)
-            q = Q[WAVES[gi][2] == 'H']
-            q.wait_ge(arrive, sum((inc[p] for p in grp)))
+            q = Q[STORE_Q[gi]]
+            q.wait_ge(A[gi], sum((inc[p] for p in grp)))
             q.dma_start(T.y[lo * R:hi * R, :], T.d[lo:hi]).then_inc(T.sem.st, 16)
             stores += 1
-    if is_root:
+    for gi, grp in enumerate(my):
+        if core == ROOT:
+            g.wait_ge(L[gi], 16)
+        else:
+            g.wait_ge(A[WAVE_OF[grp[0]]], sum((inc[p] for p in grp)))
+        calls = []
+        for p, dsts, m, e in transfers(core, grp, kids):
+            ids = []
+            for d in dsts:
+                rid, pid = topo.addr(d, core)
+                ids.append(bass.DstId(rid=rid, pnc=pid))
+            calls.append(bass.RemoteDMATransfer(dst_ids=ids, dma_engine_mask=m, remote_sem=A[WAVE_OF[p]], srcs=[T.d[p]], dsts=[T.d[p] for d in dsts]))
+            sent += e
+        if calls:
+            g.remote_dma_fused(calls, local_sem=T.sem.sent)
+    if core == ROOT:
         g.sync.wait_ge(T.sem.sent, sent)
         g.sync.dma_start(T.y[:, :], T.x[:, :]).then_inc(T.sem.st, 16)
         stores += 1

@@ -1,20 +1,20 @@
 import concourse.bass as bass
 import comms_topo
 ROOT = 277
-P = 32
+P = 64
 W = 1024 // P
 R = 128 // P
-WAVES = ((0, 8), (8, 16), (16, 26), (26, 32))
-PATH = 'HHHHHHHH' + 'DDDDDDDD' + 'DDDDDDDDCC' + 'DDDDCC'
-STORE_Q = (1, 0, 1, 0)
-STORE_ORDER = (1, 2, 3, 0)
+WAVES = ((0, 16), (16, 24), (24, 34), (34, 44), (44, 54), (54, 64))
+PATH = 'H' * 16 + 'D' * 8 + 'DDDDDDDDCC' * 4
+STORE_Q = (1, 0, 1, 0, 1, 0)
+STORE_ORDER = (1, 2, 3, 4, 5, 0)
 HELP = (0, 1, 2, 3)
 NW = len(WAVES)
 WAVE_OF = {p: w for w, (lo, hi) in enumerate(WAVES) for p in range(lo, hi)}
 XCH = tuple((3, c) for c in range(0, 16, 2)) + tuple((2, c) for c in range(0, 16, 2) if c != 2)
 CABLED = {2: 1, 3: 0}
 SCRATCH = {'d': ('dram', [P, 128, W], 'float32')}
-SEMAPHORES = ['a0', 'a1', 'a2', 'a3', 'l0', 'l1', 'l2', 'l3', 'sent', 'st']
+SEMAPHORES = ['a0', 'a1', 'a2', 'a3', 'a4', 'a5', 'l0', 'l1', 'l2', 'l3', 'l4', 'l5', 'sent', 'st']
 
 def wc(h, c, k):
     return h * 128 + c * 8 + k
@@ -30,11 +30,11 @@ def plan():
     nx = nc = 0
     for p in range(P):
         if PATH[p] == 'C':
-            h, c, k = (2, 2, (2, 6, 3, 7)[nc])
+            h, c, k = (2, 2, (2, 6, 3, 7)[nc % 4])
             nc += 1
         else:
             h, c = XCH[nx % 15]
-            k = (2, 6)[nx // 15]
+            k = (2, 6, 3, 7)[nx // 15]
             nx += 1
         near, far = (wc(h, c, k), wc(CABLED[h], c, k))
         if PATH[p] == 'H':
@@ -76,8 +76,8 @@ def rank_program(g, core, T, topo):
             for p, dsts, m, e in transfers(src, grp, kids):
                 if core in dsts:
                     inc[p] = e
-    A = [T.sem.a0, T.sem.a1, T.sem.a2, T.sem.a3]
-    L = [T.sem.l0, T.sem.l1, T.sem.l2, T.sem.l3]
+    A = [T.sem.a0, T.sem.a1, T.sem.a2, T.sem.a3, T.sem.a4, T.sem.a5]
+    L = [T.sem.l0, T.sem.l1, T.sem.l2, T.sem.l3, T.sem.l4, T.sem.l5]
     Q = [g.sync, g.scalar]
     sent = stores = 0
     if core == ROOT:

import concourse.bass as bass
import comms_topo
ROOT = 277
P = 64
W = 1024 // P
R = 128 // P
WAVES = ((0, 16), (16, 24), (24, 34), (34, 44), (44, 54), (54, 64))
PATH = 'H' * 16 + 'D' * 8 + 'DDDDDDDDCC' * 4
STORE_Q = (1, 0, 1, 0, 1, 0)
STORE_ORDER = (1, 2, 3, 4, 5, 0)
HELP = (0, 1, 2, 3)
NW = len(WAVES)
WAVE_OF = {p: w for w, (lo, hi) in enumerate(WAVES) for p in range(lo, hi)}
XCH = tuple((3, c) for c in range(0, 16, 2)) + tuple((2, c) for c in range(0, 16, 2) if c != 2)
CABLED = {2: 1, 3: 0}
SCRATCH = {'d': ('dram', [P, 128, W], 'float32')}
SEMAPHORES = ['a0', 'a1', 'a2', 'a3', 'a4', 'a5', 'l0', 'l1', 'l2', 'l3', 'l4', 'l5', 'sent', 'st']

def wc(h, c, k):
    return h * 128 + c * 8 + k

def plan():
    kids, by = ({}, {})
    def job(core, p):
        by.setdefault(core, {}).setdefault(WAVE_OF[p], []).append(p)
    for h in range(4):
        for c in range(4):
            for p in range(P):
                job(wc(h, c, 5), p)
    nx = nc = 0
    for p in range(P):
        if PATH[p] == 'C':
            h, c, k = (2, 2, (2, 6, 3, 7)[nc % 4])
            nc += 1
        else:
            h, c = XCH[nx % 15]
            k = (2, 6, 3, 7)[nx // 15]
            nx += 1
        near, far = (wc(h, c, k), wc(CABLED[h], c, k))
        if PATH[p] == 'H':
            helper = wc(2, 2, HELP[p % 4])
            kids[ROOT, p] = [helper]
            kids[helper, p] = [near]
            job(helper, p)
        else:
            kids[ROOT, p] = [near]
        for refl, hosts, first in ((far, (1, 0), []), (near, (2, 3), [far])):
            ranks = [wc(h, c, 5) for h in hosts for c in range(4) if wc(h, c, 5) != ROOT]
            s = p % len(ranks)
            kids[refl, p] = first + ranks[s:] + ranks[:s]
            job(refl, p)
    sched = {core: [ws[w] for w in sorted(ws)] for core, ws in by.items()}
    return (kids, sched)

def transfers(core, grp, kids):
    send = [p for p in grp if kids.get((core, p))]
    off = [p for p in send if any(comms_topo.mask(core, d) != 65535 for d in kids[core, p])]
    on = [p for p in send if p not in off]
    out = []
    for ps, n, base in ((off, 8, 0), (on, 8 if off else 16, 8 if off else 0)):
        if ps:
            e = 1
            while e * 2 * len(ps) <= n:
                e *= 2
            out += [(p, kids[core, p], (1 << e) - 1 << base + i * e, e) for i, p in enumerate(ps)]
    return out

def rank_program(g, core, T, topo):
    kids, sched = plan()
    my = sched.get(core)
    if not my:
        return
    inc = {}
    for src, groups in sched.items():
        for grp in groups:
            for p, dsts, m, e in transfers(src, grp, kids):
                if core in dsts:
                    inc[p] = e
    A = [T.sem.a0, T.sem.a1, T.sem.a2, T.sem.a3, T.sem.a4, T.sem.a5]
    L = [T.sem.l0, T.sem.l1, T.sem.l2, T.sem.l3, T.sem.l4, T.sem.l5]
    Q = [g.sync, g.scalar]
    sent = stores = 0
    if core == ROOT:
        for gi, grp in enumerate(my):
            lo, hi = (grp[0], grp[-1] + 1)
            Q[gi % 2].dma_start(T.d[lo:hi], T.x[lo * R:hi * R, :]).then_inc(L[gi], 16)
    elif T.rank_of(core) is not None:
        for gi in STORE_ORDER:
            grp = my[gi]
            lo, hi = (grp[0], grp[-1] + 1)
            q = Q[STORE_Q[gi]]
            q.wait_ge(A[gi], sum((inc[p] for p in grp)))
            q.dma_start(T.y[lo * R:hi * R, :], T.d[lo:hi]).then_inc(T.sem.st, 16)
            stores += 1
    for gi, grp in enumerate(my):
        if core == ROOT:
            g.wait_ge(L[gi], 16)
        else:
            g.wait_ge(A[WAVE_OF[grp[0]]], sum((inc[p] for p in grp)))
        calls = []
        for p, dsts, m, e in transfers(core, grp, kids):
            ids = []
            for d in dsts:
                rid, pid = topo.addr(d, core)
                ids.append(bass.DstId(rid=rid, pnc=pid))
            calls.append(bass.RemoteDMATransfer(dst_ids=ids, dma_engine_mask=m, remote_sem=A[WAVE_OF[p]], srcs=[T.d[p]], dsts=[T.d[p] for d in dsts]))
            sent += e
        if calls:
            g.remote_dma_fused(calls, local_sem=T.sem.sent)
    if core == ROOT:
        g.sync.wait_ge(T.sem.sent, sent)
        g.sync.dma_start(T.y[:, :], T.x[:, :]).then_inc(T.sem.st, 16)
        stores += 1
    if sent:
        g.wait_ge(T.sem.sent, sent)
    if stores:
        g.wait_ge(T.sem.st, 16 * stores)
